import numpy as np
import ml_dtypes


def mxq(x, axis, fmt="e4m3"):
    dtype, down = {"e4m3": (ml_dtypes.float8_e4m3fn, 7), "e5m2": (ml_dtypes.float8_e5m2, 14)}[fmt]
    v = np.moveaxis(np.asarray(x, np.float32).astype(ml_dtypes.bfloat16).astype(np.float64), axis, -1)
    blocks = v.reshape(v.shape[:-1] + (-1, 32))
    amax = np.abs(blocks).max(-1, keepdims=True)
    byte = np.maximum(np.where(amax > 0, np.frexp(amax)[1] - 1 + 127, 0) - down, 1)
    scale = np.exp2(byte - 127.0)
    codes = (blocks / scale).astype(np.float32).astype(dtype).astype(np.float64)
    return np.moveaxis((codes * scale).reshape(v.shape), -1, axis)


WIDE = False


def mx_kscale(k):
    if not WIDE:
        return np.ones(k)
    levels = np.array([30, -30])
    if k % 512:
        return np.exp2(np.random.permutation(np.resize(levels, k // 32))).repeat(32)
    a = np.empty((k // 512, 16))
    for p in range(k // 512):
        a[p, :8] = np.random.permutation(np.resize(levels, 8))
        for g in range(8):
            far = levels[np.abs(levels - a[p, g]) >= 10]
            a[p, g + 8] = far[np.random.randint(len(far))]
    return np.exp2(a.ravel()).repeat(32)


def f64(x):
    return np.asarray(x).astype(np.float64)


E2M1 = np.array([0.0, 0.5, 1.0, 1.5, 2.0, 3.0, 4.0, 6.0, -0.0, -0.5, -1.0, -1.5, -2.0, -3.0, -4.0, -6.0])


def pack_weight(w, fmt):
    k, n = w.shape
    w = f64(np.asarray(w, np.float32).astype(ml_dtypes.bfloat16)).reshape(k // 32, 32, n)
    amax = np.abs(w).max(1)
    if fmt == "e4m3":
        byte = np.frexp(amax)[1] - 1 + 127 - 7
    else:
        mant, ex = np.frexp(amax / 6.0)
        byte = np.where(mant > 0.5, ex, ex - 1) + 127
    byte = np.clip(np.where(amax > 0, byte, 1), 1, 254)
    scaled = (w * np.exp2(127.0 - byte)[:, None, :]).reshape(k, n).astype(np.float32)
    by_word = np.ascontiguousarray(scaled.reshape(k // 512, 128, 4, n).transpose(0, 1, 3, 2))
    if fmt == "e4m3":
        words = by_word.astype(ml_dtypes.float8_e4m3fn).view(np.uint8)
    else:
        c = by_word.astype(ml_dtypes.float4_e2m1fn).view(np.uint8) & 0xF
        words = (c[..., 0::2] | (c[..., 1::2] << 4)).reshape(k // 512, 128, 2 * n)
    return np.ascontiguousarray(words), np.ascontiguousarray(byte.astype(np.uint8).reshape(k // 512, 16, n))


def unpack_weight(words, scales, fmt):
    g, _, n = scales.shape
    words = np.ascontiguousarray(words).reshape(g, 128, n, -1)
    if fmt == "e4m3":
        vals = words.view(ml_dtypes.float8_e4m3fn).astype(np.float64)
    else:
        nib = np.empty((g, 128, n, 4), np.uint8)
        nib[..., 0::2] = words & 0xF
        nib[..., 1::2] = words >> 4
        vals = E2M1[nib]
    vals = vals * np.repeat(np.exp2(scales.astype(np.float64) - 127.0), 8, axis=1)[..., None]
    return vals.transpose(0, 1, 3, 2).reshape(g * 512, n)


H, D, T = 512, 1536, 1024


def setup_inputs():
    n = np.random.standard_normal
    s = mx_kscale(H)[:, None]
    p_wg = pack_weight(n((H, D)) / np.sqrt(H) / s, "e2m1")
    p_wu = pack_weight(n((H, D)) / np.sqrt(H) / s, "e4m3")
    return {
        "g": n((H, T)).astype(np.float32),
        "u": n((H, T)).astype(np.float32),
        "dh": (np.exp(0.5 * n((1, T))) * n((H, T)) * s).astype(np.float32),
        "wg_words": p_wg[0],
        "wg_scales": p_wg[1],
        "wu_words": p_wu[0],
        "wu_scales": p_wu[1],
        "r": (n((1024, 1536))).astype(np.float32),
    }


def reference(g, u, dh, wg_words, wg_scales, wu_words, wu_scales, r):
    sg = 1.0 / (1.0 + np.exp(-f64(g)))
    dg_ = mxq(f64(dh) * f64(u) * sg * (1.0 + f64(g) * (1.0 - sg)), 0, "e5m2")
    du_ = mxq(f64(dh) * f64(g) * sg, 0, "e5m2")
    wg_ = unpack_weight(wg_words, wg_scales, "e2m1")
    wu_ = unpack_weight(wu_words, wu_scales, "e4m3")
    y = dg_.T @ wg_ + du_.T @ wu_
    return f64(r) + y

@@ -1,0 +1,164 @@
+from contextlib import ExitStack
+
+import concourse.mybir as mybir
+
+H, D, T = 512, 1536, 1024
+FLOPS = 2 * 2 * H * D * T
+
+F32 = mybir.dt.float32
+BF16 = mybir.dt.bfloat16
+I32 = mybir.dt.int32
+U32 = mybir.dt.uint32
+U8 = mybir.dt.uint8
+E5M2 = mybir.dt.float8_e5m2_x4
+E4M3 = mybir.dt.float8_e4m3fn_x4
+E2M1 = mybir.dt.float4_e2m1fn_x4
+ACT = mybir.ActivationFunctionType
+ALU = mybir.AluOpType
+
+P = 128
+PACK = 4
+BANK = 512
+BANKS = D // BANK
+CHUNK = 256
+CHUNKS = T // CHUNK
+TILES = T // P
+HALF = T // 2
+
+
+def tile_mix_glubwd_tm_res_kernel(tc, g, u, dh, wg_words, wg_scales, wu_words, wu_scales, r, out):
+    nc = tc.nc
+    g_rows = g.rearrange("(p j) t -> p j t", j=PACK)
+    u_rows = u.rearrange("(p j) t -> p j t", j=PACK)
+    dh_rows = dh.rearrange("(p j) t -> p j t", j=PACK)
+
+    with ExitStack() as ctx:
+        keep = ctx.enter_context(tc.tile_pool(name="keep", bufs=1))
+        psum = ctx.enter_context(tc.psum_pool(name="psum", bufs=8))
+        ctx.enter_context(tc.manual_schedule())
+
+        w_planes = keep.tile([P, 2 * D], U8, align_bytes=64)
+        nc.vector.memset(w_planes[:].bitcast(U32), 0)
+        for first, scales in ((0, wg_scales), (D, wu_scales)):
+            for q in range(4):
+                nc.gpsimd.dma_start(
+                    out=w_planes[32 * q : 32 * q + 4, first : first + D].bitcast(I32),
+                    in_=scales[0][4 * q : 4 * q + 4, :].bitcast(I32),
+                )
+
+        g_sb = keep.tile([P, PACK, T], F32)
+        dh_sb = keep.tile([P, PACK, T], F32)
+        for j in range(PACK):
+            nc.sync.dma_start(out=g_sb[:, j, :], in_=g_rows[:, j, :])
+            nc.sync.dma_start(out=dh_sb[:, j, :], in_=dh_rows[:, j, :])
+        u_sb = []
+        for h in range(2):
+            u_half = keep.tile([P, PACK, HALF], F32, name="u%d" % h)
+            nc.sync.dma_start(out=u_half[:], in_=u_rows[:, :, h * HALF : (h + 1) * HALF])
+            u_sb.append(u_half)
+        wg_sb = keep.tile([P, 2 * D], U8, align_bytes=64)
+        nc.sync.dma_start(out=wg_sb[:].bitcast(I32), in_=wg_words[0].bitcast(I32))
+        wu_sb = keep.tile([P, D], U32, align_bytes=64)
+        nc.sync.dma_start(out=wu_sb[:].bitcast(I32), in_=wu_words[0].rearrange("p d i -> p (d i)").bitcast(I32))
+        rows = []
+        for i in range(TILES):
+            row = keep.tile([P, D], F32, name="row%d" % i)
+            nc.sync.dma_start(out=row[:], in_=r[i * P : (i + 1) * P, :])
+            rows.append(row)
+
+        dhs = keep.tile([P, PACK, T], F32)
+        du_bf = keep.tile([P, PACK, T], BF16)
+        for j in range(PACK):
+            nc.scalar.activation(out=dhs[:, j, :], in_=g_sb[:, j, :], func=ACT.Sigmoid)
+            halves = [slice(h * HALF, (h + 1) * HALF) for h in range(2)]
+            for cols in halves:
+                nc.vector.tensor_tensor(out=dhs[:, j, cols], in0=dh_sb[:, j, cols], in1=dhs[:, j, cols], op=ALU.mult)
+            for cols in halves:
+                nc.vector.tensor_tensor(out=du_bf[:, j, cols], in0=dhs[:, j, cols], in1=g_sb[:, j, cols], op=ALU.mult)
+
+        factor = [keep.tile([P, PACK, CHUNK], F32, name="factor%d" % c) for c in range(CHUNKS)]
+        dg_bf = [keep.tile([P, PACK, CHUNK], BF16, name="dg_bf%d" % c) for c in range(CHUNKS)]
+        grouped = {}
+        codes = {}
+        planes = {}
+        for key in ("dg", "du"):
+            for c in range(CHUNKS):
+                grouped[key, c] = keep.tile([P, CHUNK, PACK], BF16, align_bytes=64, name="grouped_%s%d" % (key, c))
+                codes[key, c] = keep.tile([P, CHUNK], U32, align_bytes=64, name="codes_%s%d" % (key, c))
+                planes[key, c] = keep.tile([P, CHUNK], U8, align_bytes=64, name="plane_%s%d" % (key, c))
+
+        def chunk_cols(c):
+            return slice(c * CHUNK, (c + 1) * CHUNK)
+
+        def silu_neg(c):
+            nc.scalar.activation(out=factor[c][:], in_=g_sb[:, :, chunk_cols(c)], func=ACT.Silu, scale=-1.0)
+
+        def times_u(c):
+            first = (c * CHUNK) % HALF
+            nc.vector.scalar_tensor_tensor(
+                out=factor[c][:], in0=factor[c][:], scalar=1.0,
+                in1=u_sb[c * CHUNK // HALF][:, :, first : first + CHUNK], op0=ALU.subtract, op1=ALU.mult,
+            )
+
+        def make_dg(c):
+            nc.vector.scalar_tensor_tensor(
+                out=dg_bf[c][:], in0=factor[c][:], scalar=-1.0,
+                in1=dhs[:, :, chunk_cols(c)], op0=ALU.mult, op1=ALU.mult,
+            )
+
+        def interleave(key, c):
+            src = dg_bf[c][:] if key == "dg" else du_bf[:, :, chunk_cols(c)]
+            nc.scalar.copy(
+                out=grouped[key, c][:].rearrange("p (c i) j -> p c j i", i=4),
+                in_=src.rearrange("p j (c i) -> p c j i", i=4),
+            )
+
+        def quantise(c):
+            for key in ("du", "dg"):
+                nc.vector.quantize_mx(
+                    out=codes[key, c][:].bitcast(E5M2), scales=planes[key, c][:],
+                    in_=grouped[key, c][:].rearrange("p t j -> p (t j)"),
+                )
+
+        def token_tile(i):
+            c, first = divmod(i * P, CHUNK)
+            tokens = slice(first, first + P)
+            for b in range(BANKS):
+                cols = slice(b * BANK, (b + 1) * BANK)
+                acc = psum.tile([P, BANK], F32, name="acc")
+                nc.tensor.matmul_mx(
+                    out=acc[:], lhsT=codes["du", c][:, tokens].bitcast(E5M2), lhsT_scale=planes["du", c][:, tokens],
+                    rhs=wu_sb[:, cols].bitcast(E4M3), rhs_scale=w_planes[:, D + b * BANK : D + (b + 1) * BANK],
+                    start=True, stop=False,
+                )
+                nc.tensor.matmul_mx(
+                    out=acc[:], lhsT=codes["dg", c][:, tokens].bitcast(E5M2), lhsT_scale=planes["dg", c][:, tokens],
+                    rhs=wg_sb[:, 2 * b * BANK : 2 * (b + 1) * BANK].bitcast(E2M1), rhs_scale=w_planes[:, cols],
+                    start=False, stop=True,
+                )
+                nc.vector.tensor_tensor(out=rows[i][:, cols], in0=acc[:], in1=rows[i][:, cols], op=ALU.add)
+            nc.sync.dma_start(out=out[i * P : (i + 1) * P, :], in_=rows[i][:])
+
+        silu_neg(0)
+        times_u(0)
+        silu_neg(1)
+        times_u(1)
+        make_dg(0)
+        interleave("du", 0)
+        silu_neg(2)
+        times_u(2)
+        make_dg(1)
+        interleave("dg", 0)
+        quantise(0)
+        silu_neg(3)
+        times_u(3)
+        make_dg(2)
+        make_dg(3)
+        for c in range(1, CHUNKS):
+            interleave("du", c)
+            interleave("dg", c)
+            quantise(c)
+            token_tile(2 * c - 2)
+            token_tile(2 * c - 1)
+        token_tile(TILES - 2)
+        token_tile(TILES - 1)

@@ -39,31 +39,36 @@ def tile_mix_glubwd_tm_res_kernel(tc, g, u, dh, wg_words, wg_scales, wu_words, w
 
         w_planes = keep.tile([P, 2 * D], U8, align_bytes=64)
         nc.vector.memset(w_planes[:].bitcast(U32), 0)
-        for first, scales in ((0, wg_scales), (D, wu_scales)):
-            for q in range(4):
-                nc.gpsimd.dma_start(
+
+        def load_scale_rows(q):
+            for first, scales in ((0, wg_scales), (D, wu_scales)):
+                nc.sync.dma_start(
                     out=w_planes[32 * q : 32 * q + 4, first : first + D].bitcast(I32),
                     in_=scales[0][4 * q : 4 * q + 4, :].bitcast(I32),
                 )
 
         g_sb = keep.tile([P, PACK, T], F32)
         dh_sb = keep.tile([P, PACK, T], F32)
-        for j in range(PACK):
-            nc.sync.dma_start(out=g_sb[:, j, :], in_=g_rows[:, j, :])
-            nc.sync.dma_start(out=dh_sb[:, j, :], in_=dh_rows[:, j, :])
-        u_sb = []
-        for h in range(2):
-            u_half = keep.tile([P, PACK, HALF], F32, name="u%d" % h)
-            nc.sync.dma_start(out=u_half[:], in_=u_rows[:, :, h * HALF : (h + 1) * HALF])
-            u_sb.append(u_half)
+        u_sb = keep.tile([P, PACK, T], F32)
+        nc.sync.dma_start(out=g_sb[:, 0:2, :], in_=g_rows[:, 0:2, :])
+        nc.sync.dma_start(out=dh_sb[:, 0:2, :], in_=dh_rows[:, 0:2, :])
+        load_scale_rows(0)
+        nc.sync.dma_start(out=g_sb[:, 2:4, :], in_=g_rows[:, 2:4, :])
+        load_scale_rows(1)
+        nc.sync.dma_start(out=dh_sb[:, 2:4, :], in_=dh_rows[:, 2:4, :])
+        load_scale_rows(2)
+        nc.sync.dma_start(out=u_sb[:], in_=u_rows)
+        load_scale_rows(3)
         wg_sb = keep.tile([P, 2 * D], U8, align_bytes=64)
         nc.sync.dma_start(out=wg_sb[:].bitcast(I32), in_=wg_words[0].bitcast(I32))
         wu_sb = keep.tile([P, D], U32, align_bytes=64)
         nc.sync.dma_start(out=wu_sb[:].bitcast(I32), in_=wu_words[0].rearrange("p d i -> p (d i)").bitcast(I32))
         rows = []
-        for i in range(TILES):
-            row = keep.tile([P, D], F32, name="row%d" % i)
-            nc.sync.dma_start(out=row[:], in_=r[i * P : (i + 1) * P, :])
+        r_rows = r.rearrange("(c m e) d -> c m e d", m=P, e=2)
+        out_rows = out.rearrange("(c m e) d -> c m e d", m=P, e=2)
+        for c in range(CHUNKS):
+            row = keep.tile([P, 2, D], F32, name="row%d" % c)
+            nc.sync.dma_start(out=row[:], in_=r_rows[c])
             rows.append(row)
 
         dhs = keep.tile([P, PACK, T], F32)
@@ -83,7 +88,7 @@ def tile_mix_glubwd_tm_res_kernel(tc, g, u, dh, wg_words, wg_scales, wu_words, w
         planes = {}
         for key in ("dg", "du"):
             for c in range(CHUNKS):
-                grouped[key, c] = keep.tile([P, CHUNK, PACK], BF16, align_bytes=64, name="grouped_%s%d" % (key, c))
+                grouped[key, c] = keep.tile([P, 2, P, PACK], BF16, align_bytes=64, name="grouped_%s%d" % (key, c))
                 codes[key, c] = keep.tile([P, CHUNK], U32, align_bytes=64, name="codes_%s%d" % (key, c))
                 planes[key, c] = keep.tile([P, CHUNK], U8, align_bytes=64, name="plane_%s%d" % (key, c))
 
@@ -94,10 +99,9 @@ def tile_mix_glubwd_tm_res_kernel(tc, g, u, dh, wg_words, wg_scales, wu_words, w
             nc.scalar.activation(out=factor[c][:], in_=g_sb[:, :, chunk_cols(c)], func=ACT.Silu, scale=-1.0)
 
         def times_u(c):
-            first = (c * CHUNK) % HALF
             nc.vector.scalar_tensor_tensor(
                 out=factor[c][:], in0=factor[c][:], scalar=1.0,
-                in1=u_sb[c * CHUNK // HALF][:, :, first : first + CHUNK], op0=ALU.subtract, op1=ALU.mult,
+                in1=u_sb[:, :, chunk_cols(c)], op0=ALU.subtract, op1=ALU.mult,
             )
 
         def make_dg(c):
@@ -109,20 +113,20 @@ def tile_mix_glubwd_tm_res_kernel(tc, g, u, dh, wg_words, wg_scales, wu_words, w
         def interleave(key, c):
             src = dg_bf[c][:] if key == "dg" else du_bf[:, :, chunk_cols(c)]
             nc.scalar.copy(
-                out=grouped[key, c][:].rearrange("p (c i) j -> p c j i", i=4),
-                in_=src.rearrange("p j (c i) -> p c j i", i=4),
+                out=grouped[key, c][:].rearrange("p e (n i) j -> p n j i e", i=2),
+                in_=src.rearrange("p j (n i e) -> p n j i e", i=2, e=2),
             )
 
         def quantise(c):
             for key in ("du", "dg"):
                 nc.vector.quantize_mx(
                     out=codes[key, c][:].bitcast(E5M2), scales=planes[key, c][:],
-                    in_=grouped[key, c][:].rearrange("p t j -> p (t j)"),
+                    in_=grouped[key, c][:].rearrange("p e m j -> p (e m j)"),
                 )
 
         def token_tile(i):
-            c, first = divmod(i * P, CHUNK)
-            tokens = slice(first, first + P)
+            c, e = divmod(i, 2)
+            tokens = slice(e * P, (e + 1) * P)
             for b in range(BANKS):
                 cols = slice(b * BANK, (b + 1) * BANK)
                 acc = psum.tile([P, BANK], F32, name="acc")
@@ -136,8 +140,11 @@ def tile_mix_glubwd_tm_res_kernel(tc, g, u, dh, wg_words, wg_scales, wu_words, w
                     rhs=wg_sb[:, 2 * b * BANK : 2 * (b + 1) * BANK].bitcast(E2M1), rhs_scale=w_planes[:, cols],
                     start=False, stop=True,
                 )
-                nc.vector.tensor_tensor(out=rows[i][:, cols], in0=acc[:], in1=rows[i][:, cols], op=ALU.add)
-            nc.sync.dma_start(out=out[i * P : (i + 1) * P, :], in_=rows[i][:])
+                nc.vector.tensor_tensor(out=rows[c][:, e, cols], in0=acc[:], in1=rows[c][:, e, cols], op=ALU.add)
+            if c >= 2:
+                nc.sync.dma_start(out=out_rows[c][:, e, :], in_=rows[c][:, e, :])
+            elif e == 1:
+                nc.sync.dma_start(out=out_rows[c], in_=rows[c][:])
 
         silu_neg(0)
         times_u(0)

@@ -43,26 +43,29 @@ def tile_mix_glubwd_tm_res_kernel(tc, g, u, dh, wg_words, wg_scales, wu_words, w
         def load_scale_rows(q):
             for first, scales in ((0, wg_scales), (D, wu_scales)):
                 nc.sync.dma_start(
-                    out=w_planes[32 * q : 32 * q + 4, first : first + D].bitcast(I32),
-                    in_=scales[0][4 * q : 4 * q + 4, :].bitcast(I32),
+                    out=w_planes[q:P:32, first : first + D].bitcast(I32),
+                    in_=scales[0][q:16:4, :].bitcast(I32),
                 )
 
         g_sb = keep.tile([P, PACK, T], F32)
         dh_sb = keep.tile([P, PACK, T], F32)
         u_sb = keep.tile([P, PACK, T], F32)
         nc.sync.dma_start(out=g_sb[:, 0:2, :], in_=g_rows[:, 0:2, :])
-        nc.sync.dma_start(out=dh_sb[:, 0:2, :], in_=dh_rows[:, 0:2, :])
-        load_scale_rows(0)
+        nc.sync.dma_start(out=dh_sb[:, 0, :], in_=dh_rows[:, 0, :])
+        nc.sync.dma_start(out=dh_sb[:, 1, :], in_=dh_rows[:, 1, :])
         nc.sync.dma_start(out=g_sb[:, 2:4, :], in_=g_rows[:, 2:4, :])
+        load_scale_rows(0)
+        nc.sync.dma_start(out=dh_sb[:, 2, :], in_=dh_rows[:, 2, :])
+        nc.sync.dma_start(out=dh_sb[:, 3, :], in_=dh_rows[:, 3, :])
         load_scale_rows(1)
-        nc.sync.dma_start(out=dh_sb[:, 2:4, :], in_=dh_rows[:, 2:4, :])
+        nc.sync.dma_start(out=u_sb[:, 0:2, :], in_=u_rows[:, 0:2, :])
         load_scale_rows(2)
-        nc.sync.dma_start(out=u_sb[:], in_=u_rows)
+        nc.sync.dma_start(out=u_sb[:, 2:4, :], in_=u_rows[:, 2:4, :])
         load_scale_rows(3)
-        wg_sb = keep.tile([P, 2 * D], U8, align_bytes=64)
-        nc.sync.dma_start(out=wg_sb[:].bitcast(I32), in_=wg_words[0].bitcast(I32))
         wu_sb = keep.tile([P, D], U32, align_bytes=64)
         nc.sync.dma_start(out=wu_sb[:].bitcast(I32), in_=wu_words[0].rearrange("p d i -> p (d i)").bitcast(I32))
+        wg_sb = keep.tile([P, 2 * D], U8, align_bytes=64)
+        nc.sync.dma_start(out=wg_sb[:].bitcast(I32), in_=wg_words[0].bitcast(I32))
         rows = []
         r_rows = r.rearrange("(c m e) d -> c m e d", m=P, e=2)
         out_rows = out.rearrange("(c m e) d -> c m e d", m=P, e=2)
@@ -81,7 +84,7 @@ def tile_mix_glubwd_tm_res_kernel(tc, g, u, dh, wg_words, wg_scales, wu_words, w
             for cols in halves:
                 nc.vector.tensor_tensor(out=du_bf[:, j, cols], in0=dhs[:, j, cols], in1=g_sb[:, j, cols], op=ALU.mult)
 
-        factor = [keep.tile([P, PACK, CHUNK], F32, name="factor%d" % c) for c in range(CHUNKS)]
+        factor = keep.tile([P, PACK, T], F32)
         dg_bf = [keep.tile([P, PACK, CHUNK], BF16, name="dg_bf%d" % c) for c in range(CHUNKS)]
         grouped = {}
         codes = {}
@@ -95,18 +98,9 @@ def tile_mix_glubwd_tm_res_kernel(tc, g, u, dh, wg_words, wg_scales, wu_words, w
         def chunk_cols(c):
             return slice(c * CHUNK, (c + 1) * CHUNK)
 
-        def silu_neg(c):
-            nc.scalar.activation(out=factor[c][:], in_=g_sb[:, :, chunk_cols(c)], func=ACT.Silu, scale=-1.0)
-
-        def times_u(c):
-            nc.vector.scalar_tensor_tensor(
-                out=factor[c][:], in0=factor[c][:], scalar=1.0,
-                in1=u_sb[:, :, chunk_cols(c)], op0=ALU.subtract, op1=ALU.mult,
-            )
-
         def make_dg(c):
             nc.vector.scalar_tensor_tensor(
-                out=dg_bf[c][:], in0=factor[c][:], scalar=-1.0,
+                out=dg_bf[c][:], in0=factor[:, :, chunk_cols(c)], scalar=-1.0,
                 in1=dhs[:, :, chunk_cols(c)], op0=ALU.mult, op1=ALU.mult,
             )
 
@@ -117,55 +111,89 @@ def tile_mix_glubwd_tm_res_kernel(tc, g, u, dh, wg_words, wg_scales, wu_words, w
                 in_=src.rearrange("p j (n i e) -> p n j i e", i=2, e=2),
             )
 
-        def quantise(c):
-            for key in ("du", "dg"):
-                nc.vector.quantize_mx(
-                    out=codes[key, c][:].bitcast(E5M2), scales=planes[key, c][:],
-                    in_=grouped[key, c][:].rearrange("p e m j -> p (e m j)"),
-                )
+        def quantise(key, c):
+            nc.vector.quantize_mx(
+                out=codes[key, c][:].bitcast(E5M2), scales=planes[key, c][:],
+                in_=grouped[key, c][:].rearrange("p e m j -> p (e m j)"),
+            )
 
-        def token_tile(i):
+        sums = {}
+
+        def place(n):
+            i, b = divmod(n, BANKS)
             c, e = divmod(i, 2)
-            tokens = slice(e * P, (e + 1) * P)
-            for b in range(BANKS):
-                cols = slice(b * BANK, (b + 1) * BANK)
-                acc = psum.tile([P, BANK], F32, name="acc")
-                nc.tensor.matmul_mx(
-                    out=acc[:], lhsT=codes["du", c][:, tokens].bitcast(E5M2), lhsT_scale=planes["du", c][:, tokens],
-                    rhs=wu_sb[:, cols].bitcast(E4M3), rhs_scale=w_planes[:, D + b * BANK : D + (b + 1) * BANK],
-                    start=True, stop=False,
-                )
-                nc.tensor.matmul_mx(
-                    out=acc[:], lhsT=codes["dg", c][:, tokens].bitcast(E5M2), lhsT_scale=planes["dg", c][:, tokens],
-                    rhs=wg_sb[:, 2 * b * BANK : 2 * (b + 1) * BANK].bitcast(E2M1), rhs_scale=w_planes[:, cols],
-                    start=False, stop=True,
-                )
-                nc.vector.tensor_tensor(out=rows[c][:, e, cols], in0=acc[:], in1=rows[c][:, e, cols], op=ALU.add)
-            if c >= 2:
-                nc.sync.dma_start(out=out_rows[c][:, e, :], in_=rows[c][:, e, :])
-            elif e == 1:
-                nc.sync.dma_start(out=out_rows[c], in_=rows[c][:])
+            return c, e, b
 
-        silu_neg(0)
-        times_u(0)
-        silu_neg(1)
-        times_u(1)
-        make_dg(0)
+        def open_sum(n):
+            c, e, b = place(n)
+            tokens = slice(e * P, (e + 1) * P)
+            sums[n] = psum.tile([P, BANK], F32, name="acc")
+            nc.tensor.matmul_mx(
+                out=sums[n][:], lhsT=codes["du", c][:, tokens].bitcast(E5M2), lhsT_scale=planes["du", c][:, tokens],
+                rhs=wu_sb[:, b * BANK : (b + 1) * BANK].bitcast(E4M3),
+                rhs_scale=w_planes[:, D + b * BANK : D + (b + 1) * BANK],
+                start=True, stop=False,
+            )
+
+        def close_sum(n):
+            c, e, b = place(n)
+            tokens = slice(e * P, (e + 1) * P)
+            nc.tensor.matmul_mx(
+                out=sums[n][:], lhsT=codes["dg", c][:, tokens].bitcast(E5M2), lhsT_scale=planes["dg", c][:, tokens],
+                rhs=wg_sb[:, 2 * b * BANK : 2 * (b + 1) * BANK].bitcast(E2M1),
+                rhs_scale=w_planes[:, b * BANK : (b + 1) * BANK],
+                start=False, stop=True,
+            )
+
+        def add_residual(n):
+            c, e, b = place(n)
+            cols = slice(b * BANK, (b + 1) * BANK)
+            nc.vector.tensor_tensor(out=rows[c][:, e, cols], in0=sums[n][:], in1=rows[c][:, e, cols], op=ALU.add)
+
+        for j in range(PACK):
+            nc.scalar.activation(out=factor[:, j, :], in_=g_sb[:, j, :], func=ACT.Silu, scale=-1.0)
+            nc.vector.scalar_tensor_tensor(
+                out=factor[:, j, :], in0=factor[:, j, :], scalar=1.0, in1=u_sb[:, j, :],
+                op0=ALU.subtract, op1=ALU.mult,
+            )
+
+        per_chunk = 2 * BANKS
         interleave("du", 0)
-        silu_neg(2)
-        times_u(2)
+        quantise("du", 0)
+        for n in range(per_chunk):
+            open_sum(n)
+        make_dg(0)
         make_dg(1)
-        interleave("dg", 0)
-        quantise(0)
-        silu_neg(3)
-        times_u(3)
+        interleave("du", 1)
+        quantise("du", 1)
+        for n in range(per_chunk, 8):
+            open_sum(n)
         make_dg(2)
+        interleave("dg", 0)
+        quantise("dg", 0)
+        for n in range(per_chunk):
+            close_sum(n)
         make_dg(3)
-        for c in range(1, CHUNKS):
+        interleave("dg", 1)
+        quantise("dg", 1)
+        for n in range(per_chunk, 8):
+            close_sum(n)
+        for c in range(2, CHUNKS):
             interleave("du", c)
             interleave("dg", c)
-            quantise(c)
-            token_tile(2 * c - 2)
-            token_tile(2 * c - 1)
-        token_tile(TILES - 2)
-        token_tile(TILES - 1)
+        for n in range(CHUNKS * per_chunk):
+            c = n // per_chunk
+            add_residual(n)
+            if n % per_chunk == BANKS - 1 and c + 2 < CHUNKS:
+                quantise("du", c + 2)
+                quantise("dg", c + 2)
+            if n + 8 < CHUNKS * per_chunk:
+                open_sum(n + 8)
+                close_sum(n + 8)
+            if c == CHUNKS - 1 and n % BANKS == BANKS - 1:
+                e = place(n)[1]
+                queue = nc.sync if e == 0 else nc.scalar
+                queue.dma_start(out=out_rows[c][:, e, :], in_=rows[c][:, e, :])
+            elif n % per_chunk == per_chunk - 1:
+                queue = nc.scalar if c % 2 == 0 else nc.sync
+                queue.dma_start(out=out_rows[c], in_=rows[c][:])

from contextlib import ExitStack

import concourse.mybir as mybir

H, D, T = 512, 1536, 1024
FLOPS = 2 * 2 * H * D * T

F32 = mybir.dt.float32
BF16 = mybir.dt.bfloat16
I32 = mybir.dt.int32
U32 = mybir.dt.uint32
U8 = mybir.dt.uint8
E5M2 = mybir.dt.float8_e5m2_x4
E4M3 = mybir.dt.float8_e4m3fn_x4
E2M1 = mybir.dt.float4_e2m1fn_x4
ACT = mybir.ActivationFunctionType
ALU = mybir.AluOpType

P = 128
PACK = 4
BANK = 512
BANKS = D // BANK
CHUNK = 256
CHUNKS = T // CHUNK
TILES = T // P
HALF = T // 2


def tile_mix_glubwd_tm_res_kernel(tc, g, u, dh, wg_words, wg_scales, wu_words, wu_scales, r, out):
    nc = tc.nc
    g_rows = g.rearrange("(p j) t -> p j t", j=PACK)
    u_rows = u.rearrange("(p j) t -> p j t", j=PACK)
    dh_rows = dh.rearrange("(p j) t -> p j t", j=PACK)

    with ExitStack() as ctx:
        keep = ctx.enter_context(tc.tile_pool(name="keep", bufs=1))
        psum = ctx.enter_context(tc.psum_pool(name="psum", bufs=8))
        ctx.enter_context(tc.manual_schedule())

        w_planes = keep.tile([P, 2 * D], U8, align_bytes=64)
        nc.vector.memset(w_planes[:].bitcast(U32), 0)

        def load_scale_rows(q):
            for first, scales in ((0, wg_scales), (D, wu_scales)):
                nc.sync.dma_start(
                    out=w_planes[q:P:32, first : first + D].bitcast(I32),
                    in_=scales[0][q:16:4, :].bitcast(I32),
                )

        g_sb = keep.tile([P, PACK, T], F32)
        dh_sb = keep.tile([P, PACK, T], F32)
        u_sb = keep.tile([P, PACK, T], F32)
        nc.sync.dma_start(out=g_sb[:, 0:2, :], in_=g_rows[:, 0:2, :])
        nc.sync.dma_start(out=dh_sb[:, 0, :], in_=dh_rows[:, 0, :])
        nc.sync.dma_start(out=dh_sb[:, 1, :], in_=dh_rows[:, 1, :])
        nc.sync.dma_start(out=g_sb[:, 2:4, :], in_=g_rows[:, 2:4, :])
        load_scale_rows(0)
        nc.sync.dma_start(out=dh_sb[:, 2, :], in_=dh_rows[:, 2, :])
        nc.sync.dma_start(out=dh_sb[:, 3, :], in_=dh_rows[:, 3, :])
        load_scale_rows(1)
        nc.sync.dma_start(out=u_sb[:, 0:2, :], in_=u_rows[:, 0:2, :])
        load_scale_rows(2)
        nc.sync.dma_start(out=u_sb[:, 2:4, :], in_=u_rows[:, 2:4, :])
        load_scale_rows(3)
        wu_sb = keep.tile([P, D], U32, align_bytes=64)
        nc.sync.dma_start(out=wu_sb[:].bitcast(I32), in_=wu_words[0].rearrange("p d i -> p (d i)").bitcast(I32))
        wg_sb = keep.tile([P, 2 * D], U8, align_bytes=64)
        nc.sync.dma_start(out=wg_sb[:].bitcast(I32), in_=wg_words[0].bitcast(I32))
        rows = []
        r_rows = r.rearrange("(c m e) d -> c m e d", m=P, e=2)
        out_rows = out.rearrange("(c m e) d -> c m e d", m=P, e=2)
        for c in range(CHUNKS):
            row = keep.tile([P, 2, D], F32, name="row%d" % c)
            nc.sync.dma_start(out=row[:], in_=r_rows[c])
            rows.append(row)

        dhs = keep.tile([P, PACK, T], F32)
        du_bf = keep.tile([P, PACK, T], BF16)
        for j in range(PACK):
            nc.scalar.activation(out=dhs[:, j, :], in_=g_sb[:, j, :], func=ACT.Sigmoid)
            halves = [slice(h * HALF, (h + 1) * HALF) for h in range(2)]
            for cols in halves:
                nc.vector.tensor_tensor(out=dhs[:, j, cols], in0=dh_sb[:, j, cols], in1=dhs[:, j, cols], op=ALU.mult)
            for cols in halves:
                nc.vector.tensor_tensor(out=du_bf[:, j, cols], in0=dhs[:, j, cols], in1=g_sb[:, j, cols], op=ALU.mult)

        factor = keep.tile([P, PACK, T], F32)
        dg_bf = [keep.tile([P, PACK, CHUNK], BF16, name="dg_bf%d" % c) for c in range(CHUNKS)]
        grouped = {}
        codes = {}
        planes = {}
        for key in ("dg", "du"):
            for c in range(CHUNKS):
                grouped[key, c] = keep.tile([P, 2, P, PACK], BF16, align_bytes=64, name="grouped_%s%d" % (key, c))
                codes[key, c] = keep.tile([P, CHUNK], U32, align_bytes=64, name="codes_%s%d" % (key, c))
                planes[key, c] = keep.tile([P, CHUNK], U8, align_bytes=64, name="plane_%s%d" % (key, c))

        def chunk_cols(c):
            return slice(c * CHUNK, (c + 1) * CHUNK)

        def make_dg(c):
            nc.vector.scalar_tensor_tensor(
                out=dg_bf[c][:], in0=factor[:, :, chunk_cols(c)], scalar=-1.0,
                in1=dhs[:, :, chunk_cols(c)], op0=ALU.mult, op1=ALU.mult,
            )

        def interleave(key, c):
            src = dg_bf[c][:] if key == "dg" else du_bf[:, :, chunk_cols(c)]
            nc.scalar.copy(
                out=grouped[key, c][:].rearrange("p e (n i) j -> p n j i e", i=2),
                in_=src.rearrange("p j (n i e) -> p n j i e", i=2, e=2),
            )

        def quantise(key, c):
            nc.vector.quantize_mx(
                out=codes[key, c][:].bitcast(E5M2), scales=planes[key, c][:],
                in_=grouped[key, c][:].rearrange("p e m j -> p (e m j)"),
            )

        sums = {}

        def place(n):
            i, b = divmod(n, BANKS)
            c, e = divmod(i, 2)
            return c, e, b

        def open_sum(n):
            c, e, b = place(n)
            tokens = slice(e * P, (e + 1) * P)
            sums[n] = psum.tile([P, BANK], F32, name="acc")
            nc.tensor.matmul_mx(
                out=sums[n][:], lhsT=codes["du", c][:, tokens].bitcast(E5M2), lhsT_scale=planes["du", c][:, tokens],
                rhs=wu_sb[:, b * BANK : (b + 1) * BANK].bitcast(E4M3),
                rhs_scale=w_planes[:, D + b * BANK : D + (b + 1) * BANK],
                start=True, stop=False,
            )

        def close_sum(n):
            c, e, b = place(n)
            tokens = slice(e * P, (e + 1) * P)
            nc.tensor.matmul_mx(
                out=sums[n][:], lhsT=codes["dg", c][:, tokens].bitcast(E5M2), lhsT_scale=planes["dg", c][:, tokens],
                rhs=wg_sb[:, 2 * b * BANK : 2 * (b + 1) * BANK].bitcast(E2M1),
                rhs_scale=w_planes[:, b * BANK : (b + 1) * BANK],
                start=False, stop=True,
            )

        def add_residual(n):
            c, e, b = place(n)
            cols = slice(b * BANK, (b + 1) * BANK)
            nc.vector.tensor_tensor(out=rows[c][:, e, cols], in0=sums[n][:], in1=rows[c][:, e, cols], op=ALU.add)

        for j in range(PACK):
            nc.scalar.activation(out=factor[:, j, :], in_=g_sb[:, j, :], func=ACT.Silu, scale=-1.0)
            nc.vector.scalar_tensor_tensor(
                out=factor[:, j, :], in0=factor[:, j, :], scalar=1.0, in1=u_sb[:, j, :],
                op0=ALU.subtract, op1=ALU.mult,
            )

        per_chunk = 2 * BANKS
        interleave("du", 0)
        quantise("du", 0)
        for n in range(per_chunk):
            open_sum(n)
        make_dg(0)
        make_dg(1)
        interleave("du", 1)
        quantise("du", 1)
        for n in range(per_chunk, 8):
            open_sum(n)
        make_dg(2)
        interleave("dg", 0)
        quantise("dg", 0)
        for n in range(per_chunk):
            close_sum(n)
        make_dg(3)
        interleave("dg", 1)
        quantise("dg", 1)
        for n in range(per_chunk, 8):
            close_sum(n)
        for c in range(2, CHUNKS):
            interleave("du", c)
            interleave("dg", c)
        for n in range(CHUNKS * per_chunk):
            c = n // per_chunk
            add_residual(n)
            if n % per_chunk == BANKS - 1 and c + 2 < CHUNKS:
                quantise("du", c + 2)
                quantise("dg", c + 2)
            if n + 8 < CHUNKS * per_chunk:
                open_sum(n + 8)
                close_sum(n + 8)
            if c == CHUNKS - 1 and n % BANKS == BANKS - 1:
                e = place(n)[1]
                queue = nc.sync if e == 0 else nc.scalar
                queue.dma_start(out=out_rows[c][:, e, :], in_=rows[c][:, e, :])
            elif n % per_chunk == per_chunk - 1:
                queue = nc.scalar if c % 2 == 0 else nc.sync
                queue.dma_start(out=out_rows[c], in_=rows[c][:])
